import numpy as np
import ml_dtypes


def mxq(x, axis, fmt="e4m3"):
    dtype, down = {"e4m3": (ml_dtypes.float8_e4m3fn, 7), "e5m2": (ml_dtypes.float8_e5m2, 14)}[fmt]
    v = np.moveaxis(np.asarray(x, np.float32).astype(ml_dtypes.bfloat16).astype(np.float64), axis, -1)
    blocks = v.reshape(v.shape[:-1] + (-1, 32))
    amax = np.abs(blocks).max(-1, keepdims=True)
    byte = np.maximum(np.where(amax > 0, np.frexp(amax)[1] - 1 + 127, 0) - down, 1)
    scale = np.exp2(byte - 127.0)
    codes = (blocks / scale).astype(np.float32).astype(dtype).astype(np.float64)
    return np.moveaxis((codes * scale).reshape(v.shape), -1, axis)


WIDE = False


def mx_kscale(k):
    if not WIDE:
        return np.ones(k)
    levels = np.array([10, -10, 5, -5, 0])
    if k % 512:
        return np.exp2(np.random.permutation(np.resize(levels, k // 32))).repeat(32)
    a = np.empty((k // 512, 16))
    for p in range(k // 512):
        a[p, :8] = np.random.permutation(np.resize(levels, 8))
        for g in range(8):
            far = levels[np.abs(levels - a[p, g]) >= 10]
            a[p, g + 8] = far[np.random.randint(len(far))]
    return np.exp2(a.ravel()).repeat(32)


def f64(x):
    return np.asarray(x).astype(np.float64)


def striped(idx):
    return np.tile(idx.reshape(-1, 16).T, (8, 1)).astype(np.uint16)


def unstriped(offs):
    return offs[:16].T.reshape(-1).astype(np.int64)


def striped8(idx):
    return np.concatenate([v.reshape(-1, 16).T for v in idx]).astype(np.uint16)


def unstriped8(offs):
    return np.stack([offs[16 * g:16 * g + 16].T.reshape(-1) for g in range(8)]).astype(np.int64)


E2M1 = np.array([0.0, 0.5, 1.0, 1.5, 2.0, 3.0, 4.0, 6.0, -0.0, -0.5, -1.0, -1.5, -2.0, -3.0, -4.0, -6.0])


def pack_weight(w, fmt):
    k, n = w.shape
    w = f64(np.asarray(w, np.float32).astype(ml_dtypes.bfloat16)).reshape(k // 32, 32, n)
    amax = np.abs(w).max(1)
    if fmt == "e4m3":
        byte = np.frexp(amax)[1] - 1 + 127 - 7
    else:
        mant, ex = np.frexp(amax / 6.0)
        byte = np.where(mant > 0.5, ex, ex - 1) + 127
    byte = np.clip(np.where(amax > 0, byte, 1), 1, 254)
    scaled = (w * np.exp2(127.0 - byte)[:, None, :]).reshape(k, n).astype(np.float32)
    by_word = np.ascontiguousarray(scaled.reshape(k // 512, 128, 4, n).transpose(0, 1, 3, 2))
    if fmt == "e4m3":
        words = by_word.astype(ml_dtypes.float8_e4m3fn).view(np.uint8)
    else:
        c = by_word.astype(ml_dtypes.float4_e2m1fn).view(np.uint8) & 0xF
        words = (c[..., 0::2] | (c[..., 1::2] << 4)).reshape(k // 512, 128, 2 * n)
    return np.ascontiguousarray(words), np.ascontiguousarray(byte.astype(np.uint8).reshape(k // 512, 16, n))


def unpack_weight(words, scales, fmt):
    g, _, n = scales.shape
    words = np.ascontiguousarray(words).reshape(g, 128, n, -1)
    if fmt == "e4m3":
        vals = words.view(ml_dtypes.float8_e4m3fn).astype(np.float64)
    else:
        nib = np.empty((g, 128, n, 4), np.uint8)
        nib[..., 0::2] = words & 0xF
        nib[..., 1::2] = words >> 4
        vals = E2M1[nib]
    vals = vals * np.repeat(np.exp2(scales.astype(np.float64) - 127.0), 8, axis=1)[..., None]
    return vals.transpose(0, 1, 3, 2).reshape(g * 512, n)


def pack_table(v):
    words, scales = pack_weight(v, "e4m3")
    return np.concatenate([words.reshape(words.shape[0], -1), scales.reshape(scales.shape[0], -1)], axis=1)


def unpack_table(tab):
    g, t = tab.shape[0], tab.shape[1] // 528
    return unpack_weight(tab[:, :512 * t].reshape(g, 128, t, 4), tab[:, 512 * t:].reshape(g, 16, t), "e4m3")


K, M, T, S = 2048, 128, 1024, 512


def setup_inputs():
    n = np.random.standard_normal
    s = mx_kscale(K)[:, None]
    s2 = mx_kscale(512)[:, None]
    p_w4 = pack_weight(n((K, M)) / np.sqrt(K) / s, "e2m1")
    return {
        "tab": pack_table(n((K, T)) * s),
        "w4_words": p_w4[0],
        "w4_scales": p_w4[1],
        "c": (n((512, S)) * s2).astype(np.float32),
        "u": (n((512, M)) / np.sqrt(512) / s2).astype(np.float32),
        "wgo": np.repeat(np.random.uniform(0.5, 2.0, (8, S)), 16, axis=0).astype(np.float32),
        "offs": striped(np.random.permutation(T)[:S]),
        "offs2": striped8(np.stack([np.random.permutation(T)[:S] for _ in range(8)])),
    }


def reference(tab, w4_words, w4_scales, c, u, wgo, offs, offs2):
    tab_ = unpack_table(tab)[:, unstriped(offs)]
    w4_ = unpack_weight(w4_words, w4_scales, "e2m1")
    c_ = mxq(f64(c), 0, "e4m3")
    u_ = mxq(f64(u), 0, "e4m3")
    y = w4_.T @ tab_ + u_.T @ c_
    place = unstriped8(offs2)[np.arange(M) % 128 // 16]
    out = np.zeros((M, T))
    out[np.arange(M)[:, None], place] = f64(wgo)[np.arange(M) % 128] * (y)
    return out

@@ -1,0 +1,162 @@
+from contextlib import ExitStack
+
+import concourse.mybir as mybir
+
+K, M, T, S, L = 2048, 128, 1024, 512, 512
+FLOPS = 2 * (K + L) * M * S
+
+F32 = mybir.dt.float32
+BF16 = mybir.dt.bfloat16
+I32 = mybir.dt.int32
+U32 = mybir.dt.uint32
+U16 = mybir.dt.uint16
+U8 = mybir.dt.uint8
+FP8X4 = mybir.dt.float8_e4m3fn_x4
+FP4X4 = mybir.dt.float4_e2m1fn_x4
+MULT = mybir.AluOpType.mult
+
+P = 128
+PASSES = K // 512
+HALF = S // 2
+GROUP = 128
+GROUPS = S // GROUP
+SHIFT_ROWS = 112
+
+
+def tile_list_tabhs_d_none_kernel(tc, tab, w4_words, w4_scales, c, u, wgo, offs, offs2, out):
+    nc = tc.nc
+    with ExitStack() as ctx:
+        keep = ctx.enter_context(tc.tile_pool(name="keep", bufs=1))
+        psum = ctx.enter_context(tc.psum_pool(name="psum", bufs=1))
+
+        pick = keep.tile([P, S // 16], U16, name="pick")
+        place = keep.tile([P, S // 16], U16, name="place")
+        scale_rows = keep.tile([P, T // 4], I32, name="scale_rows", tag="late_table", align_bytes=64)
+        words = [keep.tile([P, T], I32, name=f"words{a}", align_bytes=64) for a in range(PASSES - 1)]
+        picked_words = [keep.tile([P, S], U32, name=f"picked_words{a}", align_bytes=64) for a in range(PASSES)]
+        picked_scales = keep.tile([P, S], U8, name="picked_scales", align_bytes=64)
+        moved_scales = keep.tile([P, PASSES - 1, S // 4], I32, name="moved_scales", align_bytes=64)
+        w4 = keep.tile([P, PASSES, M // 2], I32, name="w4", align_bytes=64)
+        w4_planes = keep.tile([P, PASSES, M], U8, name="w4_planes", align_bytes=64)
+        u_raw = keep.tile([P, 4, M], F32, name="u_raw")
+        u_bf = keep.tile([P, M, 4], BF16, name="u_bf", align_bytes=64)
+        u_codes = keep.tile([P, M], U32, name="u_codes", align_bytes=64)
+        u_plane = keep.tile([P, M], U8, name="u_plane", align_bytes=64)
+        c_raw = [keep.tile([P, 4, HALF], F32, name=f"c_raw{h}") for h in range(2)]
+        c_bf = [keep.tile([P, HALF, 4], BF16, name=f"c_bf{h}", align_bytes=64) for h in range(2)]
+        c_codes = [keep.tile([P, HALF], U32, name=f"c_codes{h}", align_bytes=64) for h in range(2)]
+        c_plane = [keep.tile([P, HALF], U8, name=f"c_plane{h}", align_bytes=64) for h in range(2)]
+        sums = [keep.tile([P, HALF], F32, name=f"sums{h}") for h in range(2)]
+        placed = keep.tile([P, T], F32, name="placed")
+        warm_in = keep.tile([P, 8], F32, name="warm_in")
+        warm_out = keep.tile([P, 8], BF16, name="warm_out")
+        acc = [psum.tile([M, GROUP], F32, name=f"acc{g}") for g in range(GROUPS)]
+
+        def load_words(a):
+            nc.sync.dma_start(words[a][:], tab[a, 0 : 512 * T].rearrange("(p w) -> p w", p=P).bitcast(I32))
+
+        def load_c(h):
+            nc.sync.dma_start(c_raw[h][:], c[:, h * HALF : (h + 1) * HALF].rearrange("(p i) w -> p i w", i=4))
+
+        def interleave(dst, src):
+            nc.scalar.copy(dst[:].rearrange("p (w e) i -> p w i e", e=4), src[:].rearrange("p i (w e) -> p w i e", e=4))
+
+        def quantize(codes, plane, src):
+            nc.vector.quantize_mx(out=codes[:].bitcast(FP8X4), scales=plane[:], in_=src[:].rearrange("p w i -> p (w i)"))
+
+        def gather_words(a, lo, hi):
+            nc.vector.tensor_copy(picked_words[a][:, lo:hi], words[a][:].bitcast(U32).indirect(pick[:, lo // 16 : hi // 16]))
+
+        def table_pass(a, g, start, stop):
+            cols = slice(g * GROUP, (g + 1) * GROUP)
+            plane = picked_scales[:] if a == 0 else moved_scales[:, a - 1, :].bitcast(U8)
+            nc.tensor.matmul_mx(
+                out=acc[g][:],
+                lhsT=w4[:, a, :].bitcast(U8).bitcast(FP4X4),
+                lhsT_scale=w4_planes[:, a, :],
+                rhs=picked_words[a][:, cols].bitcast(FP8X4),
+                rhs_scale=plane[:, cols],
+                start=start,
+                stop=stop,
+            )
+
+        def feature_pass(g, start):
+            h, lo = divmod(g * GROUP, HALF)
+            nc.tensor.matmul_mx(
+                out=acc[g][:],
+                lhsT=u_codes[:].bitcast(FP8X4),
+                lhsT_scale=u_plane[:],
+                rhs=c_codes[h][:, lo : lo + GROUP].bitcast(FP8X4),
+                rhs_scale=c_plane[h][:, lo : lo + GROUP],
+                start=start,
+                stop=False,
+            )
+
+        nc.vector.memset(scale_rows[:], 0)
+        nc.vector.memset(u_raw[:, 0, 0:1], 0.0)
+        nc.vector.memset(c_raw[0][:, 0, 0:1], 0.0)
+        nc.vector.memset(words[1][:, 0:1], 0)
+        nc.vector.memset(c_raw[1][:, 0, 0:1], 0.0)
+        nc.vector.memset(w4[:, 0, 0:1], 0)
+        nc.vector.memset(words[2][:, 0:1], 0)
+        nc.vector.memset(warm_in[:], 0.0)
+        nc.scalar.copy(warm_out[:], warm_in[:])
+        nc.vector.memset(moved_scales[:], 0)
+        nc.vector.memset(placed[:], 0.0)
+        nc.gpsimd.memset(w4_planes[:], 0)
+
+        nc.sync.dma_start(pick[:], offs)
+        load_words(0)
+        nc.sync.dma_start(place[:], offs2)
+        for q in range(4):
+            rows = tab[:, 512 * T + 4 * q * T : 512 * T + 4 * (q + 1) * T].bitcast(I32)
+            nc.sync.dma_start(scale_rows[32 * q : 32 * q + 16, :], rows.rearrange("a (r t) -> a r t", r=4))
+        nc.sync.dma_start(u_raw[:], u.rearrange("(p i) n -> p i n", i=4))
+        load_c(0)
+        load_words(1)
+        load_c(1)
+        nc.sync.dma_start(w4[:], w4_words.rearrange("a p b -> p a b").bitcast(I32))
+        load_words(2)
+        for q in range(4):
+            nc.gpsimd.dma_start(
+                w4_planes[32 * q : 32 * q + 4, :, :].bitcast(I32),
+                w4_scales[:, 4 * q : 4 * q + 4, :].rearrange("a r n -> r a n").bitcast(I32),
+            )
+
+        gather_words(0, 0, S)
+        nc.vector.tensor_copy(picked_scales[:], scale_rows[:].bitcast(U8).indirect(pick[:]))
+        for a in range(1, PASSES):
+            nc.sync.dma_start(
+                moved_scales[0:SHIFT_ROWS, a - 1, :],
+                picked_scales[4 * a : 4 * a + SHIFT_ROWS, :].bitcast(I32),
+            )
+        words.append(keep.tile([P, T], I32, name="words3", tag="late_table", align_bytes=64))
+        load_words(3)
+        interleave(u_bf, u_raw)
+        interleave(c_bf[0], c_raw[0])
+        weights = keep.tile([P, S], F32, name="weights", tag="c_raw0")
+        nc.sync.dma_start(weights[:], wgo)
+        interleave(c_bf[1], c_raw[1])
+        quantize(u_codes, u_plane, u_bf)
+        gather_words(1, 0, S)
+        quantize(c_codes[0], c_plane[0], c_bf[0])
+        quantize(c_codes[1], c_plane[1], c_bf[1])
+        gather_words(2, 0, S)
+        for g in range(GROUPS):
+            feature_pass(g, True)
+        for a in range(PASSES - 1):
+            for g in range(GROUPS):
+                table_pass(a, g, False, False)
+        for g in range(GROUPS):
+            h, lo = divmod(g * GROUP, HALF)
+            gather_words(PASSES - 1, g * GROUP, (g + 1) * GROUP)
+            table_pass(PASSES - 1, g, False, True)
+            nc.scalar.copy(sums[h][:, lo : lo + GROUP], acc[g][:])
+        for h in range(2):
+            nc.vector.tensor_tensor(
+                placed[:].indirect(place[:, h * HALF // 16 : (h + 1) * HALF // 16]),
+                sums[h][:],
+                weights[:, h * HALF : (h + 1) * HALF],
+                MULT,
+            )
+        nc.sync.dma_start(out, placed[:])

@@ -37,12 +37,12 @@ def tile_list_tabhs_d_none_kernel(tc, tab, w4_words, w4_scales, c, u, wgo, offs,
         picked_scales = keep.tile([P, S], U8, name="picked_scales", align_bytes=64)
         moved_scales = keep.tile([P, PASSES - 1, S // 4], I32, name="moved_scales", align_bytes=64)
         w4 = keep.tile([P, PASSES, M // 2], I32, name="w4", align_bytes=64)
-        w4_planes = keep.tile([P, PASSES, M], U8, name="w4_planes", align_bytes=64)
+        w4_planes = keep.tile([P, PASSES, M // 4], I32, name="w4_planes", align_bytes=64)
         u_raw = keep.tile([P, 4, M], F32, name="u_raw")
         u_bf = keep.tile([P, M, 4], BF16, name="u_bf", align_bytes=64)
         u_codes = keep.tile([P, M], U32, name="u_codes", align_bytes=64)
         u_plane = keep.tile([P, M], U8, name="u_plane", align_bytes=64)
-        c_raw = [keep.tile([P, 4, HALF], F32, name=f"c_raw{h}") for h in range(2)]
+        c_raw = keep.tile([P, 4, S], F32, name="c_raw")
         c_bf = [keep.tile([P, HALF, 4], BF16, name=f"c_bf{h}", align_bytes=64) for h in range(2)]
         c_codes = [keep.tile([P, HALF], U32, name=f"c_codes{h}", align_bytes=64) for h in range(2)]
         c_plane = [keep.tile([P, HALF], U8, name=f"c_plane{h}", align_bytes=64) for h in range(2)]
@@ -55,11 +55,8 @@ def tile_list_tabhs_d_none_kernel(tc, tab, w4_words, w4_scales, c, u, wgo, offs,
         def load_words(a):
             nc.sync.dma_start(words[a][:], tab[a, 0 : 512 * T].rearrange("(p w) -> p w", p=P).bitcast(I32))
 
-        def load_c(h):
-            nc.sync.dma_start(c_raw[h][:], c[:, h * HALF : (h + 1) * HALF].rearrange("(p i) w -> p i w", i=4))
-
-        def interleave(dst, src):
-            nc.scalar.copy(dst[:].rearrange("p (w e) i -> p w i e", e=4), src[:].rearrange("p i (w e) -> p w i e", e=4))
+        def interleave(copy, dst, src):
+            copy(dst[:].rearrange("p (w e) i -> p w i e", e=4), src.rearrange("p i (w e) -> p w i e", e=4))
 
         def quantize(codes, plane, src):
             nc.vector.quantize_mx(out=codes[:].bitcast(FP8X4), scales=plane[:], in_=src[:].rearrange("p w i -> p (w i)"))
@@ -67,13 +64,19 @@ def tile_list_tabhs_d_none_kernel(tc, tab, w4_words, w4_scales, c, u, wgo, offs,
         def gather_words(a, lo, hi):
             nc.vector.tensor_copy(picked_words[a][:, lo:hi], words[a][:].bitcast(U32).indirect(pick[:, lo // 16 : hi // 16]))
 
+        def shift_scales(a):
+            nc.sync.dma_start(
+                moved_scales[0:SHIFT_ROWS, a - 1, :],
+                picked_scales[4 * a : 4 * a + SHIFT_ROWS, :].bitcast(I32),
+            )
+
         def table_pass(a, g, start, stop):
             cols = slice(g * GROUP, (g + 1) * GROUP)
             plane = picked_scales[:] if a == 0 else moved_scales[:, a - 1, :].bitcast(U8)
             nc.tensor.matmul_mx(
                 out=acc[g][:],
                 lhsT=w4[:, a, :].bitcast(U8).bitcast(FP4X4),
-                lhsT_scale=w4_planes[:, a, :],
+                lhsT_scale=w4_planes[:, a, :].bitcast(U8),
                 rhs=picked_words[a][:, cols].bitcast(FP8X4),
                 rhs_scale=plane[:, cols],
                 start=start,
@@ -94,9 +97,8 @@ def tile_list_tabhs_d_none_kernel(tc, tab, w4_words, w4_scales, c, u, wgo, offs,
 
         nc.vector.memset(scale_rows[:], 0)
         nc.vector.memset(u_raw[:, 0, 0:1], 0.0)
-        nc.vector.memset(c_raw[0][:, 0, 0:1], 0.0)
+        nc.vector.memset(c_raw[:, 0, 0:1], 0.0)
         nc.vector.memset(words[1][:, 0:1], 0)
-        nc.vector.memset(c_raw[1][:, 0, 0:1], 0.0)
         nc.vector.memset(w4[:, 0, 0:1], 0)
         nc.vector.memset(words[2][:, 0:1], 0)
         nc.vector.memset(warm_in[:], 0.0)
@@ -107,51 +109,60 @@ def tile_list_tabhs_d_none_kernel(tc, tab, w4_words, w4_scales, c, u, wgo, offs,
 
         nc.sync.dma_start(pick[:], offs)
         load_words(0)
-        nc.sync.dma_start(place[:], offs2)
         for q in range(4):
             rows = tab[:, 512 * T + 4 * q * T : 512 * T + 4 * (q + 1) * T].bitcast(I32)
             nc.sync.dma_start(scale_rows[32 * q : 32 * q + 16, :], rows.rearrange("a (r t) -> a r t", r=4))
         nc.sync.dma_start(u_raw[:], u.rearrange("(p i) n -> p i n", i=4))
-        load_c(0)
+        nc.sync.dma_start(c_raw[:], c.rearrange("(p i) w -> p i w", i=4))
         load_words(1)
-        load_c(1)
         nc.sync.dma_start(w4[:], w4_words.rearrange("a p b -> p a b").bitcast(I32))
         load_words(2)
+        nc.sync.dma_start(place[:], offs2)
         for q in range(4):
             nc.gpsimd.dma_start(
-                w4_planes[32 * q : 32 * q + 4, :, :].bitcast(I32),
+                w4_planes[32 * q : 32 * q + 4, :, :],
                 w4_scales[:, 4 * q : 4 * q + 4, :].rearrange("a r n -> r a n").bitcast(I32),
             )
 
         gather_words(0, 0, S)
         nc.vector.tensor_copy(picked_scales[:], scale_rows[:].bitcast(U8).indirect(pick[:]))
-        for a in range(1, PASSES):
-            nc.sync.dma_start(
-                moved_scales[0:SHIFT_ROWS, a - 1, :],
-                picked_scales[4 * a : 4 * a + SHIFT_ROWS, :].bitcast(I32),
-            )
+        shift_scales(1)
         words.append(keep.tile([P, T], I32, name="words3", tag="late_table", align_bytes=64))
         load_words(3)
-        interleave(u_bf, u_raw)
-        interleave(c_bf[0], c_raw[0])
-        weights = keep.tile([P, S], F32, name="weights", tag="c_raw0")
-        nc.sync.dma_start(weights[:], wgo)
-        interleave(c_bf[1], c_raw[1])
+        shift_scales(2)
+        shift_scales(3)
+        interleave(nc.scalar.copy, u_bf, u_raw[:])
+        interleave(nc.scalar.copy, c_bf[0], c_raw[:, :, 0:HALF])
         quantize(u_codes, u_plane, u_bf)
+        interleave(nc.vector.tensor_copy, c_bf[1], c_raw[:, :, HALF:S])
+        weights = keep.tile([P, S], F32, name="weights", tag="c_raw")
+        nc.sync.dma_start(weights[:], wgo)
         gather_words(1, 0, S)
-        quantize(c_codes[0], c_plane[0], c_bf[0])
         quantize(c_codes[1], c_plane[1], c_bf[1])
+        quantize(c_codes[0], c_plane[0], c_bf[0])
         gather_words(2, 0, S)
-        for g in range(GROUPS):
-            feature_pass(g, True)
-        for a in range(PASSES - 1):
-            for g in range(GROUPS):
-                table_pass(a, g, False, False)
-        for g in range(GROUPS):
+        first, second = (0, 1), (2, 3)
+
+        def last_pass(g):
             h, lo = divmod(g * GROUP, HALF)
-            gather_words(PASSES - 1, g * GROUP, (g + 1) * GROUP)
             table_pass(PASSES - 1, g, False, True)
             nc.scalar.copy(sums[h][:, lo : lo + GROUP], acc[g][:])
+
+        for g in second + first:
+            feature_pass(g, True)
+        for a in (0, 1):
+            for g in first + second:
+                table_pass(a, g, False, False)
+        for g in first:
+            table_pass(2, g, False, False)
+        for g in first:
+            gather_words(PASSES - 1, g * GROUP, (g + 1) * GROUP)
+            last_pass(g)
+        gather_words(PASSES - 1, HALF, S)
+        for g in second:
+            table_pass(2, g, False, False)
+        for g in second:
+            last_pass(g)
         for h in range(2):
             nc.vector.tensor_tensor(
                 placed[:].indirect(place[:, h * HALF // 16 : (h + 1) * HALF // 16]),

@@ -20,7 +20,6 @@ PASSES = K // 512
 HALF = S // 2
 GROUP = 128
 GROUPS = S // GROUP
-SHIFT_ROWS = 112
 
 
 def tile_list_tabhs_d_none_kernel(tc, tab, w4_words, w4_scales, c, u, wgo, offs, offs2, out):
@@ -31,26 +30,28 @@ def tile_list_tabhs_d_none_kernel(tc, tab, w4_words, w4_scales, c, u, wgo, offs,
 
         pick = keep.tile([P, S // 16], U16, name="pick")
         place = keep.tile([P, S // 16], U16, name="place")
-        scale_rows = keep.tile([P, T // 4], I32, name="scale_rows", tag="late_table", align_bytes=64)
-        words = [keep.tile([P, T], I32, name=f"words{a}", align_bytes=64) for a in range(PASSES - 1)]
+        scale_rows = keep.tile([P, T // 4], I32, name="scale_rows", align_bytes=64)
+        words = [keep.tile([P, T], I32, name=f"words{a}", align_bytes=64) for a in range(PASSES)]
         picked_words = [keep.tile([P, S], U32, name=f"picked_words{a}", align_bytes=64) for a in range(PASSES)]
         picked_scales = keep.tile([P, S], U8, name="picked_scales", align_bytes=64)
-        moved_scales = keep.tile([P, PASSES - 1, S // 4], I32, name="moved_scales", align_bytes=64)
+        staged = keep.tile([P, (S + M) // 4], I32, name="staged", align_bytes=64)
+        planes = keep.tile([P, PASSES, (S + M) // 4], I32, name="planes", align_bytes=64)
         w4 = keep.tile([P, PASSES, M // 2], I32, name="w4", align_bytes=64)
-        w4_planes = keep.tile([P, PASSES, M // 4], I32, name="w4_planes", align_bytes=64)
         u_raw = keep.tile([P, 4, M], F32, name="u_raw")
         u_bf = keep.tile([P, M, 4], BF16, name="u_bf", align_bytes=64)
         u_codes = keep.tile([P, M], U32, name="u_codes", align_bytes=64)
         u_plane = keep.tile([P, M], U8, name="u_plane", align_bytes=64)
-        c_raw = keep.tile([P, 4, S], F32, name="c_raw")
-        c_bf = [keep.tile([P, HALF, 4], BF16, name=f"c_bf{h}", align_bytes=64) for h in range(2)]
-        c_codes = [keep.tile([P, HALF], U32, name=f"c_codes{h}", align_bytes=64) for h in range(2)]
-        c_plane = [keep.tile([P, HALF], U8, name=f"c_plane{h}", align_bytes=64) for h in range(2)]
-        sums = [keep.tile([P, HALF], F32, name=f"sums{h}") for h in range(2)]
+        c_raw = [keep.tile([P, 4, HALF], F32, name=f"c_raw{h}") for h in range(2)]
+        c_bf = [keep.tile([P, GROUP, 4], BF16, name=f"c_bf{g}", align_bytes=64) for g in range(GROUPS)]
+        c_codes = [keep.tile([P, GROUP], U32, name=f"c_codes{g}", align_bytes=64) for g in range(GROUPS)]
+        c_plane = [keep.tile([P, GROUP], U8, name=f"c_plane{g}", align_bytes=64) for g in range(GROUPS)]
+        sums = [keep.tile([P, GROUP], F32, name=f"sums{g}") for g in range(GROUPS)]
+        weights = keep.tile([P, S], F32, name="weights")
         placed = keep.tile([P, T], F32, name="placed")
         warm_in = keep.tile([P, 8], F32, name="warm_in")
         warm_out = keep.tile([P, 8], BF16, name="warm_out")
         acc = [psum.tile([M, GROUP], F32, name=f"acc{g}") for g in range(GROUPS)]
+        c_rows = c.rearrange("(p i) w -> p i w", i=4)
 
         def load_words(a):
             nc.sync.dma_start(words[a][:], tab[a, 0 : 512 * T].rearrange("(p w) -> p w", p=P).bitcast(I32))
@@ -64,110 +65,99 @@ def tile_list_tabhs_d_none_kernel(tc, tab, w4_words, w4_scales, c, u, wgo, offs,
         def gather_words(a, lo, hi):
             nc.vector.tensor_copy(picked_words[a][:, lo:hi], words[a][:].bitcast(U32).indirect(pick[:, lo // 16 : hi // 16]))
 
-        def shift_scales(a):
-            nc.sync.dma_start(
-                moved_scales[0:SHIFT_ROWS, a - 1, :],
-                picked_scales[4 * a : 4 * a + SHIFT_ROWS, :].bitcast(I32),
-            )
-
         def table_pass(a, g, start, stop):
             cols = slice(g * GROUP, (g + 1) * GROUP)
-            plane = picked_scales[:] if a == 0 else moved_scales[:, a - 1, :].bitcast(U8)
+            both = planes[:, a, :].bitcast(U8)
             nc.tensor.matmul_mx(
                 out=acc[g][:],
                 lhsT=w4[:, a, :].bitcast(U8).bitcast(FP4X4),
-                lhsT_scale=w4_planes[:, a, :].bitcast(U8),
+                lhsT_scale=both[:, S : S + M],
                 rhs=picked_words[a][:, cols].bitcast(FP8X4),
-                rhs_scale=plane[:, cols],
+                rhs_scale=both[:, cols],
                 start=start,
                 stop=stop,
             )
 
-        def feature_pass(g, start):
-            h, lo = divmod(g * GROUP, HALF)
+        def feature_pass(g, start, stop):
             nc.tensor.matmul_mx(
                 out=acc[g][:],
                 lhsT=u_codes[:].bitcast(FP8X4),
                 lhsT_scale=u_plane[:],
-                rhs=c_codes[h][:, lo : lo + GROUP].bitcast(FP8X4),
-                rhs_scale=c_plane[h][:, lo : lo + GROUP],
+                rhs=c_codes[g][:].bitcast(FP8X4),
+                rhs_scale=c_plane[g][:],
                 start=start,
-                stop=False,
+                stop=stop,
             )
 
-        nc.vector.memset(scale_rows[:], 0)
-        nc.vector.memset(u_raw[:, 0, 0:1], 0.0)
-        nc.vector.memset(c_raw[:, 0, 0:1], 0.0)
-        nc.vector.memset(words[1][:, 0:1], 0)
-        nc.vector.memset(w4[:, 0, 0:1], 0)
-        nc.vector.memset(words[2][:, 0:1], 0)
-        nc.vector.memset(warm_in[:], 0.0)
-        nc.scalar.copy(warm_out[:], warm_in[:])
-        nc.vector.memset(moved_scales[:], 0)
-        nc.vector.memset(placed[:], 0.0)
-        nc.gpsimd.memset(w4_planes[:], 0)
+        def load_c(h):
+            nc.sync.dma_start(c_raw[h][:], c_rows[:, :, h * HALF : (h + 1) * HALF])
+
+        def load_weights(lo, hi):
+            nc.sync.dma_start(weights[:, lo:hi], wgo[:, lo:hi])
+
+        def prepare_c(g, copy):
+            h, lo = divmod(g * GROUP, HALF)
+            interleave(copy, c_bf[g], c_raw[h][:, :, lo : lo + GROUP])
+            quantize(c_codes[g], c_plane[g], c_bf[g])
+
+        def place_sums(g):
+            nc.scalar.copy(sums[g][:], acc[g][:])
+            nc.vector.tensor_tensor(
+                placed[:].indirect(place[:, g * GROUP // 16 : (g + 1) * GROUP // 16]),
+                sums[g][:],
+                weights[:, g * GROUP : (g + 1) * GROUP],
+                MULT,
+            )
 
         nc.sync.dma_start(pick[:], offs)
+        nc.scalar.dma_start(
+            scale_rows[0:64, :], tab[:, 512 * T : 528 * T].bitcast(I32).rearrange("a (q t) -> q a t", q=16)
+        )
+        nc.scalar.dma_start(staged[0:64, S // 4 :], w4_scales.bitcast(I32).rearrange("a q n -> q a n"))
         load_words(0)
-        for q in range(4):
-            rows = tab[:, 512 * T + 4 * q * T : 512 * T + 4 * (q + 1) * T].bitcast(I32)
-            nc.sync.dma_start(scale_rows[32 * q : 32 * q + 16, :], rows.rearrange("a (r t) -> a r t", r=4))
-        nc.sync.dma_start(u_raw[:], u.rearrange("(p i) n -> p i n", i=4))
-        nc.sync.dma_start(c_raw[:], c.rearrange("(p i) w -> p i w", i=4))
         load_words(1)
         nc.sync.dma_start(w4[:], w4_words.rearrange("a p b -> p a b").bitcast(I32))
         load_words(2)
-        nc.sync.dma_start(place[:], offs2)
-        for q in range(4):
-            nc.gpsimd.dma_start(
-                w4_planes[32 * q : 32 * q + 4, :, :],
-                w4_scales[:, 4 * q : 4 * q + 4, :].rearrange("a r n -> r a n").bitcast(I32),
-            )
-
-        gather_words(0, 0, S)
-        nc.vector.tensor_copy(picked_scales[:], scale_rows[:].bitcast(U8).indirect(pick[:]))
-        shift_scales(1)
-        words.append(keep.tile([P, T], I32, name="words3", tag="late_table", align_bytes=64))
+        nc.sync.dma_start(u_raw[:], u.rearrange("(p i) n -> p i n", i=4))
+        load_c(0)
         load_words(3)
-        shift_scales(2)
-        shift_scales(3)
+        nc.sync.dma_start(place[:], offs2)
+        load_weights(0, GROUP)
+        load_c(1)
+        load_weights(HALF, S)
+        load_weights(GROUP, HALF)
+
+        nc.vector.memset(scale_rows[64:128, :], 0)
+        nc.vector.memset(warm_in[:], 0.0)
+        nc.scalar.copy(warm_out[:], warm_in[:])
+        nc.vector.memset(planes[:], 0)
+        nc.vector.memset(placed[:], 0.0)
+
+        nc.vector.tensor_copy(picked_scales[:], scale_rows[:].bitcast(U8).indirect(pick[:]))
+        nc.vector.tensor_copy(staged[0:64, 0 : S // 4], picked_scales[0:64, :].bitcast(I32))
+        for q in range(4):
+            nc.scalar.dma_start(planes[32 * q : 32 * q + 4, :, :], staged[16 * q : 16 * q + 16, :])
+        for a in range(PASSES - 1):
+            gather_words(a, 0, S)
         interleave(nc.scalar.copy, u_bf, u_raw[:])
-        interleave(nc.scalar.copy, c_bf[0], c_raw[:, :, 0:HALF])
         quantize(u_codes, u_plane, u_bf)
-        interleave(nc.vector.tensor_copy, c_bf[1], c_raw[:, :, HALF:S])
-        weights = keep.tile([P, S], F32, name="weights", tag="c_raw")
-        nc.sync.dma_start(weights[:], wgo)
-        gather_words(1, 0, S)
-        quantize(c_codes[1], c_plane[1], c_bf[1])
-        quantize(c_codes[0], c_plane[0], c_bf[0])
-        gather_words(2, 0, S)
-        first, second = (0, 1), (2, 3)
+        prepare_c(1, nc.vector.tensor_copy)
+        prepare_c(0, nc.scalar.copy)
 
-        def last_pass(g):
-            h, lo = divmod(g * GROUP, HALF)
-            table_pass(PASSES - 1, g, False, True)
-            nc.scalar.copy(sums[h][:, lo : lo + GROUP], acc[g][:])
-
-        for g in second + first:
-            feature_pass(g, True)
-        for a in (0, 1):
-            for g in first + second:
-                table_pass(a, g, False, False)
-        for g in first:
-            table_pass(2, g, False, False)
-        for g in first:
+        for g in (0, 1):
+            for a in range(PASSES - 1):
+                table_pass(a, g, a == 0, False)
+            feature_pass(g, False, False)
+        for g in (0, 1):
             gather_words(PASSES - 1, g * GROUP, (g + 1) * GROUP)
-            last_pass(g)
+            table_pass(PASSES - 1, g, False, True)
         gather_words(PASSES - 1, HALF, S)
-        for g in second:
-            table_pass(2, g, False, False)
-        for g in second:
-            last_pass(g)
-        for h in range(2):
-            nc.vector.tensor_tensor(
-                placed[:].indirect(place[:, h * HALF // 16 : (h + 1) * HALF // 16]),
-                sums[h][:],
-                weights[:, h * HALF : (h + 1) * HALF],
-                MULT,
-            )
+        place_sums(0)
+        for g in (2, 3):
+            prepare_c(g, nc.scalar.copy)
+            place_sums(g - 1)
+            for a in range(PASSES):
+                table_pass(a, g, a == 0, False)
+            feature_pass(g, False, True)
+        place_sums(3)
         nc.sync.dma_start(out, placed[:])

@@ -41,23 +41,24 @@ def tile_list_tabhs_d_none_kernel(tc, tab, w4_words, w4_scales, c, u, wgo, offs,
         u_bf = keep.tile([P, M, 4], BF16, name="u_bf", align_bytes=64)
         u_codes = keep.tile([P, M], U32, name="u_codes", align_bytes=64)
         u_plane = keep.tile([P, M], U8, name="u_plane", align_bytes=64)
-        c_raw = [keep.tile([P, 4, HALF], F32, name=f"c_raw{h}") for h in range(2)]
+        c_raw = [keep.tile([P, 4, GROUP], F32, name=f"c_raw{g}") for g in range(GROUPS)]
         c_bf = [keep.tile([P, GROUP, 4], BF16, name=f"c_bf{g}", align_bytes=64) for g in range(GROUPS)]
         c_codes = [keep.tile([P, GROUP], U32, name=f"c_codes{g}", align_bytes=64) for g in range(GROUPS)]
         c_plane = [keep.tile([P, GROUP], U8, name=f"c_plane{g}", align_bytes=64) for g in range(GROUPS)]
-        sums = [keep.tile([P, GROUP], F32, name=f"sums{g}") for g in range(GROUPS)]
+        last_sums = keep.tile([P, GROUP], F32, name="last_sums")
+        sums = [c_raw[g + 1][:, 0, :] for g in range(GROUPS - 1)] + [last_sums[:]]
         weights = keep.tile([P, S], F32, name="weights")
         placed = keep.tile([P, T], F32, name="placed")
         warm_in = keep.tile([P, 8], F32, name="warm_in")
         warm_out = keep.tile([P, 8], BF16, name="warm_out")
-        acc = [psum.tile([M, GROUP], F32, name=f"acc{g}") for g in range(GROUPS)]
+        acc = [psum.tile([M, GROUP], F32, name=f"acc{g}", tag=f"bank{g}") for g in range(2)]
         c_rows = c.rearrange("(p i) w -> p i w", i=4)
 
         def load_words(a):
             nc.sync.dma_start(words[a][:], tab[a, 0 : 512 * T].rearrange("(p w) -> p w", p=P).bitcast(I32))
 
-        def interleave(copy, dst, src):
-            copy(dst[:].rearrange("p (w e) i -> p w i e", e=4), src.rearrange("p i (w e) -> p w i e", e=4))
+        def interleave(dst, src):
+            nc.scalar.copy(dst[:].rearrange("p (w e) i -> p w i e", e=4), src.rearrange("p i (w e) -> p w i e", e=4))
 
         def quantize(codes, plane, src):
             nc.vector.quantize_mx(out=codes[:].bitcast(FP8X4), scales=plane[:], in_=src[:].rearrange("p w i -> p (w i)"))
@@ -89,22 +90,21 @@ def tile_list_tabhs_d_none_kernel(tc, tab, w4_words, w4_scales, c, u, wgo, offs,
                 stop=stop,
             )
 
-        def load_c(h):
-            nc.sync.dma_start(c_raw[h][:], c_rows[:, :, h * HALF : (h + 1) * HALF])
+        def load_c(g):
+            nc.sync.dma_start(c_raw[g][:], c_rows[:, :, g * GROUP : (g + 1) * GROUP])
 
         def load_weights(lo, hi):
             nc.sync.dma_start(weights[:, lo:hi], wgo[:, lo:hi])
 
-        def prepare_c(g, copy):
-            h, lo = divmod(g * GROUP, HALF)
-            interleave(copy, c_bf[g], c_raw[h][:, :, lo : lo + GROUP])
+        def prepare_c(g):
+            interleave(c_bf[g], c_raw[g][:])
             quantize(c_codes[g], c_plane[g], c_bf[g])
 
         def place_sums(g):
-            nc.scalar.copy(sums[g][:], acc[g][:])
+            nc.scalar.copy(sums[g], acc[g][:])
             nc.vector.tensor_tensor(
                 placed[:].indirect(place[:, g * GROUP // 16 : (g + 1) * GROUP // 16]),
-                sums[g][:],
+                sums[g],
                 weights[:, g * GROUP : (g + 1) * GROUP],
                 MULT,
             )
@@ -118,14 +118,6 @@ def tile_list_tabhs_d_none_kernel(tc, tab, w4_words, w4_scales, c, u, wgo, offs,
         load_words(1)
         nc.sync.dma_start(w4[:], w4_words.rearrange("a p b -> p a b").bitcast(I32))
         load_words(2)
-        nc.sync.dma_start(u_raw[:], u.rearrange("(p i) n -> p i n", i=4))
-        load_c(0)
-        load_words(3)
-        nc.sync.dma_start(place[:], offs2)
-        load_weights(0, GROUP)
-        load_c(1)
-        load_weights(HALF, S)
-        load_weights(GROUP, HALF)
 
         nc.vector.memset(scale_rows[64:128, :], 0)
         nc.vector.memset(warm_in[:], 0.0)
@@ -136,28 +128,36 @@ def tile_list_tabhs_d_none_kernel(tc, tab, w4_words, w4_scales, c, u, wgo, offs,
         nc.vector.tensor_copy(picked_scales[:], scale_rows[:].bitcast(U8).indirect(pick[:]))
         nc.vector.tensor_copy(staged[0:64, 0 : S // 4], picked_scales[0:64, :].bitcast(I32))
         for q in range(4):
-            nc.scalar.dma_start(planes[32 * q : 32 * q + 4, :, :], staged[16 * q : 16 * q + 16, :])
+            nc.sync.dma_start(planes[32 * q : 32 * q + 4, :, :], staged[16 * q : 16 * q + 16, :])
+        nc.sync.dma_start(u_raw[:], u.rearrange("(p i) n -> p i n", i=4))
+        load_c(0)
+        load_words(3)
+        load_c(1)
+        nc.sync.dma_start(place[:], offs2)
+        load_weights(0, GROUP)
+        load_c(2)
+        load_weights(GROUP, HALF)
+        load_c(3)
+        load_weights(HALF, S)
         for a in range(PASSES - 1):
             gather_words(a, 0, S)
-        interleave(nc.scalar.copy, u_bf, u_raw[:])
+        interleave(u_bf, u_raw[:])
         quantize(u_codes, u_plane, u_bf)
-        prepare_c(1, nc.vector.tensor_copy)
-        prepare_c(0, nc.scalar.copy)
+        prepare_c(0)
 
-        for g in (0, 1):
-            for a in range(PASSES - 1):
-                table_pass(a, g, a == 0, False)
-            feature_pass(g, False, False)
-        for g in (0, 1):
-            gather_words(PASSES - 1, g * GROUP, (g + 1) * GROUP)
-            table_pass(PASSES - 1, g, False, True)
-        gather_words(PASSES - 1, HALF, S)
-        place_sums(0)
-        for g in (2, 3):
-            prepare_c(g, nc.scalar.copy)
+        for a in range(PASSES - 1):
+            table_pass(a, 0, a == 0, False)
+        feature_pass(0, False, False)
+        for lo, hi in ((0, GROUP), (GROUP, S)):
+            gather_words(PASSES - 1, lo, hi)
+        table_pass(PASSES - 1, 0, False, True)
+        for g in range(1, GROUPS):
+            prepare_c(g)
             place_sums(g - 1)
+            if g >= 2:
+                acc.append(psum.tile([M, GROUP], F32, name=f"acc{g}", tag=f"bank{g - 2}"))
             for a in range(PASSES):
                 table_pass(a, g, a == 0, False)
             feature_pass(g, False, True)
-        place_sums(3)
+        place_sums(GROUPS - 1)
         nc.sync.dma_start(out, placed[:])

@@ -49,8 +49,6 @@ def tile_list_tabhs_d_none_kernel(tc, tab, w4_words, w4_scales, c, u, wgo, offs,
         sums = [c_raw[g + 1][:, 0, :] for g in range(GROUPS - 1)] + [last_sums[:]]
         weights = keep.tile([P, S], F32, name="weights")
         placed = keep.tile([P, T], F32, name="placed")
-        warm_in = keep.tile([P, 8], F32, name="warm_in")
-        warm_out = keep.tile([P, 8], BF16, name="warm_out")
         acc = [psum.tile([M, GROUP], F32, name=f"acc{g}", tag=f"bank{g}") for g in range(2)]
         c_rows = c.rearrange("(p i) w -> p i w", i=4)
 
@@ -116,12 +114,11 @@ def tile_list_tabhs_d_none_kernel(tc, tab, w4_words, w4_scales, c, u, wgo, offs,
         nc.scalar.dma_start(staged[0:64, S // 4 :], w4_scales.bitcast(I32).rearrange("a q n -> q a n"))
         load_words(0)
         load_words(1)
+        nc.sync.dma_start(u_raw[:], u.rearrange("(p i) n -> p i n", i=4))
         nc.sync.dma_start(w4[:], w4_words.rearrange("a p b -> p a b").bitcast(I32))
         load_words(2)
 
         nc.vector.memset(scale_rows[64:128, :], 0)
-        nc.vector.memset(warm_in[:], 0.0)
-        nc.scalar.copy(warm_out[:], warm_in[:])
         nc.vector.memset(planes[:], 0)
         nc.vector.memset(placed[:], 0.0)
 
@@ -129,7 +126,6 @@ def tile_list_tabhs_d_none_kernel(tc, tab, w4_words, w4_scales, c, u, wgo, offs,
         nc.vector.tensor_copy(staged[0:64, 0 : S // 4], picked_scales[0:64, :].bitcast(I32))
         for q in range(4):
             nc.sync.dma_start(planes[32 * q : 32 * q + 4, :, :], staged[16 * q : 16 * q + 16, :])
-        nc.sync.dma_start(u_raw[:], u.rearrange("(p i) n -> p i n", i=4))
         load_c(0)
         load_words(3)
         load_c(1)

@@ -45,8 +45,7 @@ def tile_list_tabhs_d_none_kernel(tc, tab, w4_words, w4_scales, c, u, wgo, offs,
         c_bf = [keep.tile([P, GROUP, 4], BF16, name=f"c_bf{g}", align_bytes=64) for g in range(GROUPS)]
         c_codes = [keep.tile([P, GROUP], U32, name=f"c_codes{g}", align_bytes=64) for g in range(GROUPS)]
         c_plane = [keep.tile([P, GROUP], U8, name=f"c_plane{g}", align_bytes=64) for g in range(GROUPS)]
-        last_sums = keep.tile([P, GROUP], F32, name="last_sums")
-        sums = [c_raw[g + 1][:, 0, :] for g in range(GROUPS - 1)] + [last_sums[:]]
+        sums = [keep.tile([P, GROUP], F32, name=f"sums{g}") for g in range(GROUPS)]
         weights = keep.tile([P, S], F32, name="weights")
         placed = keep.tile([P, T], F32, name="placed")
         acc = [psum.tile([M, GROUP], F32, name=f"acc{g}", tag=f"bank{g}") for g in range(2)]
@@ -99,13 +98,8 @@ def tile_list_tabhs_d_none_kernel(tc, tab, w4_words, w4_scales, c, u, wgo, offs,
             quantize(c_codes[g], c_plane[g], c_bf[g])
 
         def place_sums(g):
-            nc.scalar.copy(sums[g], acc[g][:])
-            nc.vector.tensor_tensor(
-                placed[:].indirect(place[:, g * GROUP // 16 : (g + 1) * GROUP // 16]),
-                sums[g],
-                weights[:, g * GROUP : (g + 1) * GROUP],
-                MULT,
-            )
+            nc.vector.tensor_tensor(sums[g][:], acc[g][:], weights[:, g * GROUP : (g + 1) * GROUP], MULT)
+            nc.vector.tensor_copy(placed[:].indirect(place[:, g * GROUP // 16 : (g + 1) * GROUP // 16]), sums[g][:])
 
         nc.sync.dma_start(pick[:], offs)
         nc.scalar.dma_start(

@@ -20,6 +20,8 @@ PASSES = K // 512
 HALF = S // 2
 GROUP = 128
 GROUPS = S // GROUP
+HEAD = 32
+LEAD = GROUP - HEAD
 
 
 def tile_list_tabhs_d_none_kernel(tc, tab, w4_words, w4_scales, c, u, wgo, offs, offs2, out):
@@ -41,21 +43,22 @@ def tile_list_tabhs_d_none_kernel(tc, tab, w4_words, w4_scales, c, u, wgo, offs,
         u_bf = keep.tile([P, M, 4], BF16, name="u_bf", align_bytes=64)
         u_codes = keep.tile([P, M], U32, name="u_codes", align_bytes=64)
         u_plane = keep.tile([P, M], U8, name="u_plane", align_bytes=64)
-        c_raw = [keep.tile([P, 4, GROUP], F32, name=f"c_raw{g}") for g in range(GROUPS)]
+        c_held = [keep.tile([P, LEAD + 4 * GROUP], F32, name=f"c_held{g}") for g in range(GROUPS)]
+        c_raw = [t[:, LEAD:].rearrange("p (i w) -> p i w", i=4) for t in c_held]
         c_bf = [keep.tile([P, GROUP, 4], BF16, name=f"c_bf{g}", align_bytes=64) for g in range(GROUPS)]
         c_codes = [keep.tile([P, GROUP], U32, name=f"c_codes{g}", align_bytes=64) for g in range(GROUPS)]
         c_plane = [keep.tile([P, GROUP], U8, name=f"c_plane{g}", align_bytes=64) for g in range(GROUPS)]
-        sums = [keep.tile([P, GROUP], F32, name=f"sums{g}") for g in range(GROUPS)]
+        last_sums = keep.tile([P, GROUP], F32, name="last_sums")
         weights = keep.tile([P, S], F32, name="weights")
         placed = keep.tile([P, T], F32, name="placed")
-        acc = [psum.tile([M, GROUP], F32, name=f"acc{g}", tag=f"bank{g}") for g in range(2)]
+        acc = [psum.tile([M, GROUP], F32, name=f"acc{g}", tag=f"bank{g}") for g in range(GROUPS - 1)]
         c_rows = c.rearrange("(p i) w -> p i w", i=4)
 
         def load_words(a):
             nc.sync.dma_start(words[a][:], tab[a, 0 : 512 * T].rearrange("(p w) -> p w", p=P).bitcast(I32))
 
         def interleave(dst, src):
-            nc.scalar.copy(dst[:].rearrange("p (w e) i -> p w i e", e=4), src.rearrange("p i (w e) -> p w i e", e=4))
+            nc.scalar.copy(dst.rearrange("p (w e) i -> p w i e", e=4), src.rearrange("p i (w e) -> p w i e", e=4))
 
         def quantize(codes, plane, src):
             nc.vector.quantize_mx(out=codes[:].bitcast(FP8X4), scales=plane[:], in_=src[:].rearrange("p w i -> p (w i)"))
@@ -88,18 +91,25 @@ def tile_list_tabhs_d_none_kernel(tc, tab, w4_words, w4_scales, c, u, wgo, offs,
             )
 
         def load_c(g):
-            nc.sync.dma_start(c_raw[g][:], c_rows[:, :, g * GROUP : (g + 1) * GROUP])
+            nc.sync.dma_start(c_raw[g], c_rows[:, :, g * GROUP : (g + 1) * GROUP])
 
         def load_weights(lo, hi):
             nc.sync.dma_start(weights[:, lo:hi], wgo[:, lo:hi])
 
         def prepare_c(g):
-            interleave(c_bf[g], c_raw[g][:])
+            for lo, hi in ((0, HEAD), (HEAD, GROUP)) if g else ((0, GROUP),):
+                interleave(c_bf[g][:, lo:hi, :], c_raw[g][:, :, lo:hi])
             quantize(c_codes[g], c_plane[g], c_bf[g])
 
         def place_sums(g):
-            nc.vector.tensor_tensor(sums[g][:], acc[g][:], weights[:, g * GROUP : (g + 1) * GROUP], MULT)
-            nc.vector.tensor_copy(placed[:].indirect(place[:, g * GROUP // 16 : (g + 1) * GROUP // 16]), sums[g][:])
+            held = c_held[g + 1][:, 0:GROUP] if g + 1 < GROUPS else last_sums[:]
+            nc.scalar.copy(held, acc[g][:])
+            nc.vector.tensor_tensor(
+                placed[:].indirect(place[:, g * GROUP // 16 : (g + 1) * GROUP // 16]),
+                held,
+                weights[:, g * GROUP : (g + 1) * GROUP],
+                MULT,
+            )
 
         nc.sync.dma_start(pick[:], offs)
         nc.scalar.dma_start(
@@ -131,12 +141,13 @@ def tile_list_tabhs_d_none_kernel(tc, tab, w4_words, w4_scales, c, u, wgo, offs,
         load_weights(HALF, S)
         for a in range(PASSES - 1):
             gather_words(a, 0, S)
-        interleave(u_bf, u_raw[:])
+        interleave(u_bf[:], u_raw[:])
         quantize(u_codes, u_plane, u_bf)
         prepare_c(0)
 
-        for a in range(PASSES - 1):
-            table_pass(a, 0, a == 0, False)
+        for g in range(GROUPS - 1):
+            for a in range(PASSES - 1):
+                table_pass(a, g, a == 0, False)
         feature_pass(0, False, False)
         for lo, hi in ((0, GROUP), (GROUP, S)):
             gather_words(PASSES - 1, lo, hi)
@@ -144,10 +155,11 @@ def tile_list_tabhs_d_none_kernel(tc, tab, w4_words, w4_scales, c, u, wgo, offs,
         for g in range(1, GROUPS):
             prepare_c(g)
             place_sums(g - 1)
-            if g >= 2:
-                acc.append(psum.tile([M, GROUP], F32, name=f"acc{g}", tag=f"bank{g - 2}"))
-            for a in range(PASSES):
-                table_pass(a, g, a == 0, False)
+            if g == GROUPS - 1:
+                acc.append(psum.tile([M, GROUP], F32, name="acc_last", tag="bank1"))
+                for a in range(PASSES - 1):
+                    table_pass(a, g, a == 0, False)
+            table_pass(PASSES - 1, g, False, False)
             feature_pass(g, False, True)
         place_sums(GROUPS - 1)
         nc.sync.dma_start(out, placed[:])

@@ -113,23 +113,24 @@ def tile_list_tabhs_d_none_kernel(tc, tab, w4_words, w4_scales, c, u, wgo, offs,
 
         nc.sync.dma_start(pick[:], offs)
         nc.scalar.dma_start(
-            scale_rows[0:64, :], tab[:, 512 * T : 528 * T].bitcast(I32).rearrange("a (q t) -> q a t", q=16)
+            scale_rows[32:96, :], tab[:, 512 * T : 528 * T].bitcast(I32).rearrange("a (q t) -> q a t", q=16)
         )
-        nc.scalar.dma_start(staged[0:64, S // 4 :], w4_scales.bitcast(I32).rearrange("a q n -> q a n"))
+        nc.scalar.dma_start(staged[32:96, S // 4 :], w4_scales.bitcast(I32).rearrange("a q n -> q a n"))
         load_words(0)
         load_words(1)
         nc.sync.dma_start(u_raw[:], u.rearrange("(p i) n -> p i n", i=4))
         nc.sync.dma_start(w4[:], w4_words.rearrange("a p b -> p a b").bitcast(I32))
         load_words(2)
 
-        nc.vector.memset(scale_rows[64:128, :], 0)
+        nc.vector.memset(scale_rows[0:32, :], 0)
+        nc.vector.memset(scale_rows[96:128, :], 0)
         nc.vector.memset(planes[:], 0)
         nc.vector.memset(placed[:], 0.0)
 
         nc.vector.tensor_copy(picked_scales[:], scale_rows[:].bitcast(U8).indirect(pick[:]))
-        nc.vector.tensor_copy(staged[0:64, 0 : S // 4], picked_scales[0:64, :].bitcast(I32))
-        for q in range(4):
-            nc.sync.dma_start(planes[32 * q : 32 * q + 4, :, :], staged[16 * q : 16 * q + 16, :])
+        nc.vector.tensor_copy(staged[:, 0 : S // 4], picked_scales[:].bitcast(I32))
+        for q in (0, 2, 1, 3):
+            nc.sync.dma_start(planes[32 * q : 32 * q + 4, :, :], staged[32 + 16 * q : 48 + 16 * q, :])
         load_c(0)
         load_words(3)
         load_c(1)

@@ -111,6 +111,7 @@ def tile_list_tabhs_d_none_kernel(tc, tab, w4_words, w4_scales, c, u, wgo, offs,
                 MULT,
             )
 
+        nc.sync.dma_start(u_raw[:], u.rearrange("(p i) n -> p i n", i=4))
         nc.sync.dma_start(pick[:], offs)
         nc.scalar.dma_start(
             scale_rows[32:96, :], tab[:, 512 * T : 528 * T].bitcast(I32).rearrange("a (q t) -> q a t", q=16)
@@ -118,7 +119,6 @@ def tile_list_tabhs_d_none_kernel(tc, tab, w4_words, w4_scales, c, u, wgo, offs,
         nc.scalar.dma_start(staged[32:96, S // 4 :], w4_scales.bitcast(I32).rearrange("a q n -> q a n"))
         load_words(0)
         load_words(1)
-        nc.sync.dma_start(u_raw[:], u.rearrange("(p i) n -> p i n", i=4))
         nc.sync.dma_start(w4[:], w4_words.rearrange("a p b -> p a b").bitcast(I32))
         load_words(2)
 

@@ -22,6 +22,7 @@ GROUP = 128
 GROUPS = S // GROUP
 HEAD = 32
 LEAD = GROUP - HEAD
+FIRST_ENTRY = (0, 3 * GROUP, GROUP, 2 * GROUP)
 
 
 def tile_list_tabhs_d_none_kernel(tc, tab, w4_words, w4_scales, c, u, wgo, offs, offs2, out):
@@ -67,7 +68,7 @@ def tile_list_tabhs_d_none_kernel(tc, tab, w4_words, w4_scales, c, u, wgo, offs,
             nc.vector.tensor_copy(picked_words[a][:, lo:hi], words[a][:].bitcast(U32).indirect(pick[:, lo // 16 : hi // 16]))
 
         def table_pass(a, g, start, stop):
-            cols = slice(g * GROUP, (g + 1) * GROUP)
+            cols = slice(FIRST_ENTRY[g], FIRST_ENTRY[g] + GROUP)
             both = planes[:, a, :].bitcast(U8)
             nc.tensor.matmul_mx(
                 out=acc[g][:],
@@ -91,7 +92,7 @@ def tile_list_tabhs_d_none_kernel(tc, tab, w4_words, w4_scales, c, u, wgo, offs,
             )
 
         def load_c(g):
-            nc.sync.dma_start(c_raw[g], c_rows[:, :, g * GROUP : (g + 1) * GROUP])
+            nc.sync.dma_start(c_raw[g], c_rows[:, :, FIRST_ENTRY[g] : FIRST_ENTRY[g] + GROUP])
 
         def load_weights(lo, hi):
             nc.sync.dma_start(weights[:, lo:hi], wgo[:, lo:hi])
@@ -105,9 +106,9 @@ def tile_list_tabhs_d_none_kernel(tc, tab, w4_words, w4_scales, c, u, wgo, offs,
             held = c_held[g + 1][:, 0:GROUP] if g + 1 < GROUPS else last_sums[:]
             nc.scalar.copy(held, acc[g][:])
             nc.vector.tensor_tensor(
-                placed[:].indirect(place[:, g * GROUP // 16 : (g + 1) * GROUP // 16]),
+                placed[:].indirect(place[:, FIRST_ENTRY[g] // 16 : (FIRST_ENTRY[g] + GROUP) // 16]),
                 held,
-                weights[:, g * GROUP : (g + 1) * GROUP],
+                weights[:, FIRST_ENTRY[g] : FIRST_ENTRY[g] + GROUP],
                 MULT,
             )
 
@@ -121,6 +122,7 @@ def tile_list_tabhs_d_none_kernel(tc, tab, w4_words, w4_scales, c, u, wgo, offs,
         load_words(1)
         nc.sync.dma_start(w4[:], w4_words.rearrange("a p b -> p a b").bitcast(I32))
         load_words(2)
+        load_c(0)
 
         nc.vector.memset(scale_rows[0:32, :], 0)
         nc.vector.memset(scale_rows[96:128, :], 0)
@@ -131,28 +133,29 @@ def tile_list_tabhs_d_none_kernel(tc, tab, w4_words, w4_scales, c, u, wgo, offs,
         nc.vector.tensor_copy(staged[:, 0 : S // 4], picked_scales[:].bitcast(I32))
         for q in (0, 2, 1, 3):
             nc.sync.dma_start(planes[32 * q : 32 * q + 4, :, :], staged[32 + 16 * q : 48 + 16 * q, :])
-        load_c(0)
         load_words(3)
         load_c(1)
         nc.sync.dma_start(place[:], offs2)
         load_weights(0, GROUP)
         load_c(2)
-        load_weights(GROUP, HALF)
+        load_weights(S - GROUP, S)
         load_c(3)
-        load_weights(HALF, S)
+        load_weights(GROUP, S - GROUP)
         for a in range(PASSES - 1):
             gather_words(a, 0, S)
         interleave(u_bf[:], u_raw[:])
         quantize(u_codes, u_plane, u_bf)
         prepare_c(0)
 
-        for g in range(GROUPS - 1):
+        for g in range(2):
             for a in range(PASSES - 1):
                 table_pass(a, g, a == 0, False)
         feature_pass(0, False, False)
-        for lo, hi in ((0, GROUP), (GROUP, S)):
+        for lo, hi in ((0, GROUP), (GROUP, HALF), (HALF, S)):
             gather_words(PASSES - 1, lo, hi)
         table_pass(PASSES - 1, 0, False, True)
+        for a in reversed(range(PASSES)):
+            table_pass(a, 2, a == PASSES - 1, False)
         for g in range(1, GROUPS):
             prepare_c(g)
             place_sums(g - 1)
@@ -160,7 +163,8 @@ def tile_list_tabhs_d_none_kernel(tc, tab, w4_words, w4_scales, c, u, wgo, offs,
                 acc.append(psum.tile([M, GROUP], F32, name="acc_last", tag="bank1"))
                 for a in range(PASSES - 1):
                     table_pass(a, g, a == 0, False)
-            table_pass(PASSES - 1, g, False, False)
+            if g != 2:
+                table_pass(PASSES - 1, g, False, False)
             feature_pass(g, False, True)
         place_sums(GROUPS - 1)
         nc.sync.dma_start(out, placed[:])

@@ -17,12 +17,10 @@ MULT = mybir.AluOpType.mult
 
 P = 128
 PASSES = K // 512
-HALF = S // 2
 GROUP = 128
 GROUPS = S // GROUP
 HEAD = 32
 LEAD = GROUP - HEAD
-FIRST_ENTRY = (0, 3 * GROUP, GROUP, 2 * GROUP)
 
 
 def tile_list_tabhs_d_none_kernel(tc, tab, w4_words, w4_scales, c, u, wgo, offs, offs2, out):
@@ -49,7 +47,7 @@ def tile_list_tabhs_d_none_kernel(tc, tab, w4_words, w4_scales, c, u, wgo, offs,
         c_bf = [keep.tile([P, GROUP, 4], BF16, name=f"c_bf{g}", align_bytes=64) for g in range(GROUPS)]
         c_codes = [keep.tile([P, GROUP], U32, name=f"c_codes{g}", align_bytes=64) for g in range(GROUPS)]
         c_plane = [keep.tile([P, GROUP], U8, name=f"c_plane{g}", align_bytes=64) for g in range(GROUPS)]
-        last_sums = keep.tile([P, GROUP], F32, name="last_sums")
+        last_sums = keep.tile([P, 2 * GROUP], F32, name="last_sums")
         weights = keep.tile([P, S], F32, name="weights")
         placed = keep.tile([P, T], F32, name="placed")
         acc = [psum.tile([M, GROUP], F32, name=f"acc{g}", tag=f"bank{g}") for g in range(GROUPS - 1)]
@@ -68,7 +66,7 @@ def tile_list_tabhs_d_none_kernel(tc, tab, w4_words, w4_scales, c, u, wgo, offs,
             nc.vector.tensor_copy(picked_words[a][:, lo:hi], words[a][:].bitcast(U32).indirect(pick[:, lo // 16 : hi // 16]))
 
         def table_pass(a, g, start, stop):
-            cols = slice(FIRST_ENTRY[g], FIRST_ENTRY[g] + GROUP)
+            cols = slice(g * GROUP, (g + 1) * GROUP)
             both = planes[:, a, :].bitcast(U8)
             nc.tensor.matmul_mx(
                 out=acc[g][:],
@@ -92,25 +90,21 @@ def tile_list_tabhs_d_none_kernel(tc, tab, w4_words, w4_scales, c, u, wgo, offs,
             )
 
         def load_c(g):
-            nc.sync.dma_start(c_raw[g], c_rows[:, :, FIRST_ENTRY[g] : FIRST_ENTRY[g] + GROUP])
+            nc.sync.dma_start(c_raw[g], c_rows[:, :, g * GROUP : (g + 1) * GROUP])
 
         def load_weights(lo, hi):
             nc.sync.dma_start(weights[:, lo:hi], wgo[:, lo:hi])
 
         def prepare_c(g):
-            for lo, hi in ((0, HEAD), (HEAD, GROUP)) if g else ((0, GROUP),):
+            for lo, hi in ((0, HEAD), (HEAD, GROUP)) if g % 2 else ((0, GROUP),):
                 interleave(c_bf[g][:, lo:hi, :], c_raw[g][:, :, lo:hi])
             quantize(c_codes[g], c_plane[g], c_bf[g])
 
-        def place_sums(g):
-            held = c_held[g + 1][:, 0:GROUP] if g + 1 < GROUPS else last_sums[:]
-            nc.scalar.copy(held, acc[g][:])
-            nc.vector.tensor_tensor(
-                placed[:].indirect(place[:, FIRST_ENTRY[g] // 16 : (FIRST_ENTRY[g] + GROUP) // 16]),
-                held,
-                weights[:, FIRST_ENTRY[g] : FIRST_ENTRY[g] + GROUP],
-                MULT,
-            )
+        def place_sums(held, groups):
+            for n, g in enumerate(groups):
+                nc.scalar.copy(held[:, n * GROUP : (n + 1) * GROUP], acc[g][:])
+            lo, hi = groups[0] * GROUP, (groups[-1] + 1) * GROUP
+            nc.vector.tensor_tensor(placed[:].indirect(place[:, lo // 16 : hi // 16]), held, weights[:, lo:hi], MULT)
 
         nc.sync.dma_start(u_raw[:], u.rearrange("(p i) n -> p i n", i=4))
         nc.sync.dma_start(pick[:], offs)
@@ -122,7 +116,6 @@ def tile_list_tabhs_d_none_kernel(tc, tab, w4_words, w4_scales, c, u, wgo, offs,
         load_words(1)
         nc.sync.dma_start(w4[:], w4_words.rearrange("a p b -> p a b").bitcast(I32))
         load_words(2)
-        load_c(0)
 
         nc.vector.memset(scale_rows[0:32, :], 0)
         nc.vector.memset(scale_rows[96:128, :], 0)
@@ -133,38 +126,38 @@ def tile_list_tabhs_d_none_kernel(tc, tab, w4_words, w4_scales, c, u, wgo, offs,
         nc.vector.tensor_copy(staged[:, 0 : S // 4], picked_scales[:].bitcast(I32))
         for q in (0, 2, 1, 3):
             nc.sync.dma_start(planes[32 * q : 32 * q + 4, :, :], staged[32 + 16 * q : 48 + 16 * q, :])
+        load_c(0)
         load_words(3)
         load_c(1)
         nc.sync.dma_start(place[:], offs2)
         load_weights(0, GROUP)
         load_c(2)
-        load_weights(S - GROUP, S)
         load_c(3)
-        load_weights(GROUP, S - GROUP)
+        load_weights(GROUP, S)
         for a in range(PASSES - 1):
             gather_words(a, 0, S)
         interleave(u_bf[:], u_raw[:])
         quantize(u_codes, u_plane, u_bf)
         prepare_c(0)
 
-        for g in range(2):
+        for g in range(GROUPS - 1):
             for a in range(PASSES - 1):
                 table_pass(a, g, a == 0, False)
         feature_pass(0, False, False)
-        for lo, hi in ((0, GROUP), (GROUP, HALF), (HALF, S)):
+        for lo, hi in ((0, GROUP), (GROUP, S)):
             gather_words(PASSES - 1, lo, hi)
         table_pass(PASSES - 1, 0, False, True)
-        for a in reversed(range(PASSES)):
-            table_pass(a, 2, a == PASSES - 1, False)
-        for g in range(1, GROUPS):
+        prepare_c(1)
+        table_pass(PASSES - 1, 1, False, False)
+        feature_pass(1, False, True)
+        table_pass(PASSES - 1, 2, False, False)
+        place_sums(c_held[1][:, 0:GROUP], (0,))
+        acc.append(psum.tile([M, GROUP], F32, name="acc_last", tag="bank0"))
+        for a in range(PASSES):
+            table_pass(a, 3, a == 0, False)
+        for g in (2, 3):
             prepare_c(g)
-            place_sums(g - 1)
-            if g == GROUPS - 1:
-                acc.append(psum.tile([M, GROUP], F32, name="acc_last", tag="bank1"))
-                for a in range(PASSES - 1):
-                    table_pass(a, g, a == 0, False)
-            if g != 2:
-                table_pass(PASSES - 1, g, False, False)
             feature_pass(g, False, True)
-        place_sums(GROUPS - 1)
+        place_sums(c_held[3][:, 0:GROUP], (1,))
+        place_sums(last_sums[:], (2, 3))
         nc.sync.dma_start(out, placed[:])

@@ -20,7 +20,9 @@ PASSES = K // 512
 GROUP = 128
 GROUPS = S // GROUP
 HEAD = 32
-LEAD = GROUP - HEAD
+MX_ALIGN = 64
+DMA_ALIGN = 256
+PLANE_BYTES = S + M
 
 
 def tile_list_tabhs_d_none_kernel(tc, tab, w4_words, w4_scales, c, u, wgo, offs, offs2, out):
@@ -29,65 +31,32 @@ def tile_list_tabhs_d_none_kernel(tc, tab, w4_words, w4_scales, c, u, wgo, offs,
         keep = ctx.enter_context(tc.tile_pool(name="keep", bufs=1))
         psum = ctx.enter_context(tc.psum_pool(name="psum", bufs=1))
 
-        pick = keep.tile([P, S // 16], U16, name="pick")
-        place = keep.tile([P, S // 16], U16, name="place")
-        scale_rows = keep.tile([P, T // 4], I32, name="scale_rows", align_bytes=64)
-        words = [keep.tile([P, T], I32, name=f"words{a}", align_bytes=64) for a in range(PASSES)]
-        picked_words = [keep.tile([P, S], U32, name=f"picked_words{a}", align_bytes=64) for a in range(PASSES)]
-        picked_scales = keep.tile([P, S], U8, name="picked_scales", align_bytes=64)
-        staged = keep.tile([P, (S + M) // 4], I32, name="staged", align_bytes=64)
-        planes = keep.tile([P, PASSES, (S + M) // 4], I32, name="planes", align_bytes=64)
-        w4 = keep.tile([P, PASSES, M // 2], I32, name="w4", align_bytes=64)
-        u_raw = keep.tile([P, 4, M], F32, name="u_raw")
-        u_bf = keep.tile([P, M, 4], BF16, name="u_bf", align_bytes=64)
-        u_codes = keep.tile([P, M], U32, name="u_codes", align_bytes=64)
-        u_plane = keep.tile([P, M], U8, name="u_plane", align_bytes=64)
-        c_held = [keep.tile([P, LEAD + 4 * GROUP], F32, name=f"c_held{g}") for g in range(GROUPS)]
-        c_raw = [t[:, LEAD:].rearrange("p (i w) -> p i w", i=4) for t in c_held]
-        c_bf = [keep.tile([P, GROUP, 4], BF16, name=f"c_bf{g}", align_bytes=64) for g in range(GROUPS)]
-        c_codes = [keep.tile([P, GROUP], U32, name=f"c_codes{g}", align_bytes=64) for g in range(GROUPS)]
-        c_plane = [keep.tile([P, GROUP], U8, name=f"c_plane{g}", align_bytes=64) for g in range(GROUPS)]
+        pick = keep.tile([P, S // 16], U16, name="pick", align_bytes=DMA_ALIGN)
+        place = keep.tile([P, S // 16], U16, name="place", align_bytes=DMA_ALIGN)
+        scale_rows = keep.tile([P, T // 4], I32, name="scale_rows", align_bytes=DMA_ALIGN)
+        words = [keep.tile([P, T], I32, name=f"words{a}", align_bytes=DMA_ALIGN) for a in range(PASSES)]
+        picked_words = [keep.tile([P, S], U32, name=f"picked_words{a}", align_bytes=MX_ALIGN) for a in range(PASSES)]
+        picked_scales = keep.tile([P, S], U8, name="picked_scales", align_bytes=MX_ALIGN)
+        staged = keep.tile([P, PLANE_BYTES // 4], I32, name="staged", align_bytes=DMA_ALIGN)
+        planes = keep.tile([P, PASSES, PLANE_BYTES // 4], I32, name="planes", align_bytes=DMA_ALIGN)
+        w4 = keep.tile([P, PASSES, M // 2], I32, name="w4", align_bytes=DMA_ALIGN)
+        u_raw = keep.tile([P, 4, M], F32, name="u_raw", align_bytes=DMA_ALIGN)
+        u_bf = keep.tile([P, M, 4], BF16, name="u_bf", align_bytes=MX_ALIGN)
+        u_codes = keep.tile([P, M], U32, name="u_codes", align_bytes=MX_ALIGN)
+        u_plane = keep.tile([P, M], U8, name="u_plane", align_bytes=MX_ALIGN)
+        c_held = [keep.tile([P, 5 * GROUP], F32, name=f"c_held{g}", align_bytes=DMA_ALIGN) for g in range(GROUPS)]
+        c_raw = [t[:, GROUP:].rearrange("p (i w) -> p i w", i=4) for t in c_held]
+        c_bf = [keep.tile([P, GROUP, 4], BF16, name=f"c_bf{g}", align_bytes=MX_ALIGN) for g in range(GROUPS)]
+        c_codes = [keep.tile([P, GROUP], U32, name=f"c_codes{g}", align_bytes=MX_ALIGN) for g in range(GROUPS)]
+        c_plane = [keep.tile([P, GROUP], U8, name=f"c_plane{g}", align_bytes=MX_ALIGN) for g in range(GROUPS)]
         last_sums = keep.tile([P, 2 * GROUP], F32, name="last_sums")
-        weights = keep.tile([P, S], F32, name="weights")
-        placed = keep.tile([P, T], F32, name="placed")
+        weights = keep.tile([P, S], F32, name="weights", align_bytes=DMA_ALIGN)
+        placed = keep.tile([P, T], F32, name="placed", align_bytes=DMA_ALIGN)
         acc = [psum.tile([M, GROUP], F32, name=f"acc{g}", tag=f"bank{g}") for g in range(GROUPS - 1)]
         c_rows = c.rearrange("(p i) w -> p i w", i=4)
 
         def load_words(a):
             nc.sync.dma_start(words[a][:], tab[a, 0 : 512 * T].rearrange("(p w) -> p w", p=P).bitcast(I32))
-
-        def interleave(dst, src):
-            nc.scalar.copy(dst.rearrange("p (w e) i -> p w i e", e=4), src.rearrange("p i (w e) -> p w i e", e=4))
-
-        def quantize(codes, plane, src):
-            nc.vector.quantize_mx(out=codes[:].bitcast(FP8X4), scales=plane[:], in_=src[:].rearrange("p w i -> p (w i)"))
-
-        def gather_words(a, lo, hi):
-            nc.vector.tensor_copy(picked_words[a][:, lo:hi], words[a][:].bitcast(U32).indirect(pick[:, lo // 16 : hi // 16]))
-
-        def table_pass(a, g, start, stop):
-            cols = slice(g * GROUP, (g + 1) * GROUP)
-            both = planes[:, a, :].bitcast(U8)
-            nc.tensor.matmul_mx(
-                out=acc[g][:],
-                lhsT=w4[:, a, :].bitcast(U8).bitcast(FP4X4),
-                lhsT_scale=both[:, S : S + M],
-                rhs=picked_words[a][:, cols].bitcast(FP8X4),
-                rhs_scale=both[:, cols],
-                start=start,
-                stop=stop,
-            )
-
-        def feature_pass(g, start, stop):
-            nc.tensor.matmul_mx(
-                out=acc[g][:],
-                lhsT=u_codes[:].bitcast(FP8X4),
-                lhsT_scale=u_plane[:],
-                rhs=c_codes[g][:].bitcast(FP8X4),
-                rhs_scale=c_plane[g][:],
-                start=start,
-                stop=stop,
-            )
 
         def load_c(g):
             nc.sync.dma_start(c_raw[g], c_rows[:, :, g * GROUP : (g + 1) * GROUP])
@@ -95,16 +64,56 @@ def tile_list_tabhs_d_none_kernel(tc, tab, w4_words, w4_scales, c, u, wgo, offs,
         def load_weights(lo, hi):
             nc.sync.dma_start(weights[:, lo:hi], wgo[:, lo:hi])
 
-        def prepare_c(g):
-            for lo, hi in ((0, HEAD), (HEAD, GROUP)) if g % 2 else ((0, GROUP),):
+        def interleave(dst, src):
+            nc.scalar.copy(dst.rearrange("p (w e) i -> p w i e", e=4), src.rearrange("p i (w e) -> p w i e", e=4))
+
+        def quantize(codes, plane, src):
+            nc.vector.quantize_mx(out=codes[:].bitcast(FP8X4), scales=plane[:], in_=src[:].rearrange("p w i -> p (w i)"))
+
+        def prepare_c(g, pieces):
+            for lo, hi in pieces:
                 interleave(c_bf[g][:, lo:hi, :], c_raw[g][:, :, lo:hi])
             quantize(c_codes[g], c_plane[g], c_bf[g])
+
+        def sums_over_head(g):
+            return c_held[g][:, HEAD : HEAD + GROUP]
+
+        def gather_words(a, lo, hi):
+            nc.vector.tensor_copy(picked_words[a][:, lo:hi], words[a][:].bitcast(U32).indirect(pick[:, lo // 16 : hi // 16]))
+
+        def table_pass(a, g, start, stop):
+            cols = slice(g * GROUP, (g + 1) * GROUP)
+            plane = planes[:, a, :].bitcast(U8)
+            nc.tensor.matmul_mx(
+                out=acc[g][:],
+                lhsT=w4[:, a, :].bitcast(U8).bitcast(FP4X4),
+                lhsT_scale=plane[:, S:PLANE_BYTES],
+                rhs=picked_words[a][:, cols].bitcast(FP8X4),
+                rhs_scale=plane[:, cols],
+                start=start,
+                stop=stop,
+            )
+
+        def feature_pass(g, stop):
+            nc.tensor.matmul_mx(
+                out=acc[g][:],
+                lhsT=u_codes[:].bitcast(FP8X4),
+                lhsT_scale=u_plane[:],
+                rhs=c_codes[g][:].bitcast(FP8X4),
+                rhs_scale=c_plane[g][:],
+                start=False,
+                stop=stop,
+            )
 
         def place_sums(held, groups):
             for n, g in enumerate(groups):
                 nc.scalar.copy(held[:, n * GROUP : (n + 1) * GROUP], acc[g][:])
             lo, hi = groups[0] * GROUP, (groups[-1] + 1) * GROUP
             nc.vector.tensor_tensor(placed[:].indirect(place[:, lo // 16 : hi // 16]), held, weights[:, lo:hi], MULT)
+
+        whole = ((0, GROUP),)
+        head_first = ((0, HEAD), (HEAD, GROUP))
+        last = PASSES - 1
 
         nc.sync.dma_start(u_raw[:], u.rearrange("(p i) n -> p i n", i=4))
         nc.sync.dma_start(pick[:], offs)
@@ -124,40 +133,44 @@ def tile_list_tabhs_d_none_kernel(tc, tab, w4_words, w4_scales, c, u, wgo, offs,
 
         nc.vector.tensor_copy(picked_scales[:], scale_rows[:].bitcast(U8).indirect(pick[:]))
         nc.vector.tensor_copy(staged[:, 0 : S // 4], picked_scales[:].bitcast(I32))
-        for q in (0, 2, 1, 3):
-            nc.sync.dma_start(planes[32 * q : 32 * q + 4, :, :], staged[32 + 16 * q : 48 + 16 * q, :])
+        for d in (0, 2, 1, 3):
+            nc.sync.dma_start(planes[32 * d : 32 * d + 4, :, :], staged[32 + 16 * d : 48 + 16 * d, :])
+
         load_c(0)
-        load_words(3)
+        load_words(last)
         load_c(1)
         nc.sync.dma_start(place[:], offs2)
         load_weights(0, GROUP)
         load_c(2)
         load_c(3)
         load_weights(GROUP, S)
-        for a in range(PASSES - 1):
+
+        for a in range(last):
             gather_words(a, 0, S)
         interleave(u_bf[:], u_raw[:])
         quantize(u_codes, u_plane, u_bf)
-        prepare_c(0)
-
+        prepare_c(0, whole)
         for g in range(GROUPS - 1):
-            for a in range(PASSES - 1):
+            for a in range(last):
                 table_pass(a, g, a == 0, False)
-        feature_pass(0, False, False)
-        for lo, hi in ((0, GROUP), (GROUP, S)):
-            gather_words(PASSES - 1, lo, hi)
-        table_pass(PASSES - 1, 0, False, True)
-        prepare_c(1)
-        table_pass(PASSES - 1, 1, False, False)
-        feature_pass(1, False, True)
-        table_pass(PASSES - 1, 2, False, False)
-        place_sums(c_held[1][:, 0:GROUP], (0,))
+        feature_pass(0, False)
+
+        gather_words(last, 0, GROUP)
+        gather_words(last, GROUP, S)
+        table_pass(last, 0, False, True)
+        prepare_c(1, head_first)
+        table_pass(last, 1, False, False)
+        feature_pass(1, True)
+        table_pass(last, 2, False, False)
+        place_sums(sums_over_head(1), (0,))
+
         acc.append(psum.tile([M, GROUP], F32, name="acc_last", tag="bank0"))
         for a in range(PASSES):
             table_pass(a, 3, a == 0, False)
-        for g in (2, 3):
-            prepare_c(g)
-            feature_pass(g, False, True)
-        place_sums(c_held[3][:, 0:GROUP], (1,))
+
+        for g, pieces in ((2, whole), (3, head_first)):
+            prepare_c(g, pieces)
+            feature_pass(g, True)
+        place_sums(sums_over_head(3), (1,))
         place_sums(last_sums[:], (2, 3))
         nc.sync.dma_start(out, placed[:])

@@ -58,8 +58,8 @@ def tile_list_tabhs_d_none_kernel(tc, tab, w4_words, w4_scales, c, u, wgo, offs,
         def load_words(a):
             nc.sync.dma_start(words[a][:], tab[a, 0 : 512 * T].rearrange("(p w) -> p w", p=P).bitcast(I32))
 
-        def load_c(g):
-            nc.sync.dma_start(c_raw[g], c_rows[:, :, g * GROUP : (g + 1) * GROUP])
+        def load_c(g, lo=0, hi=GROUP):
+            nc.sync.dma_start(c_raw[g][:, :, lo:hi], c_rows[:, :, g * GROUP + lo : g * GROUP + hi])
 
         def load_weights(lo, hi):
             nc.sync.dma_start(weights[:, lo:hi], wgo[:, lo:hi])
@@ -113,6 +113,7 @@ def tile_list_tabhs_d_none_kernel(tc, tab, w4_words, w4_scales, c, u, wgo, offs,
 
         whole = ((0, GROUP),)
         head_first = ((0, HEAD), (HEAD, GROUP))
+        halves = ((GROUP // 2, GROUP), (0, GROUP // 2))
         last = PASSES - 1
 
         nc.sync.dma_start(u_raw[:], u.rearrange("(p i) n -> p i n", i=4))
@@ -138,7 +139,8 @@ def tile_list_tabhs_d_none_kernel(tc, tab, w4_words, w4_scales, c, u, wgo, offs,
 
         load_c(0)
         load_words(last)
-        load_c(1)
+        for lo, hi in halves:
+            load_c(1, lo, hi)
         nc.sync.dma_start(place[:], offs2)
         load_weights(0, GROUP)
         load_c(2)
@@ -158,7 +160,7 @@ def tile_list_tabhs_d_none_kernel(tc, tab, w4_words, w4_scales, c, u, wgo, offs,
         gather_words(last, 0, GROUP)
         gather_words(last, GROUP, S)
         table_pass(last, 0, False, True)
-        prepare_c(1, head_first)
+        prepare_c(1, halves)
         table_pass(last, 1, False, False)
         feature_pass(1, True)
         table_pass(last, 2, False, False)

@@ -23,6 +23,7 @@ HEAD = 32
 MX_ALIGN = 64
 DMA_ALIGN = 256
 PLANE_BYTES = S + M
+PLANE_PITCH = 3 * DMA_ALIGN
 
 
 def tile_list_tabhs_d_none_kernel(tc, tab, w4_words, w4_scales, c, u, wgo, offs, offs2, out):
@@ -38,7 +39,7 @@ def tile_list_tabhs_d_none_kernel(tc, tab, w4_words, w4_scales, c, u, wgo, offs,
         picked_words = [keep.tile([P, S], U32, name=f"picked_words{a}", align_bytes=MX_ALIGN) for a in range(PASSES)]
         picked_scales = keep.tile([P, S], U8, name="picked_scales", align_bytes=MX_ALIGN)
         staged = keep.tile([P, PLANE_BYTES // 4], I32, name="staged", align_bytes=DMA_ALIGN)
-        planes = keep.tile([P, PASSES, PLANE_BYTES // 4], I32, name="planes", align_bytes=DMA_ALIGN)
+        planes = keep.tile([P, PASSES, PLANE_PITCH // 4], I32, name="planes", align_bytes=DMA_ALIGN)
         w4 = keep.tile([P, PASSES, M // 2], I32, name="w4", align_bytes=DMA_ALIGN)
         u_raw = keep.tile([P, 4, M], F32, name="u_raw", align_bytes=DMA_ALIGN)
         u_bf = keep.tile([P, M, 4], BF16, name="u_bf", align_bytes=MX_ALIGN)
@@ -129,13 +130,13 @@ def tile_list_tabhs_d_none_kernel(tc, tab, w4_words, w4_scales, c, u, wgo, offs,
 
         nc.vector.memset(scale_rows[0:32, :], 0)
         nc.vector.memset(scale_rows[96:128, :], 0)
-        nc.vector.memset(planes[:], 0)
+        nc.vector.memset(planes[:, :, 0 : PLANE_BYTES // 4], 0)
         nc.vector.memset(placed[:], 0.0)
 
         nc.vector.tensor_copy(picked_scales[:], scale_rows[:].bitcast(U8).indirect(pick[:]))
         nc.vector.tensor_copy(staged[:, 0 : S // 4], picked_scales[:].bitcast(I32))
         for d in (0, 2, 1, 3):
-            nc.sync.dma_start(planes[32 * d : 32 * d + 4, :, :], staged[32 + 16 * d : 48 + 16 * d, :])
+            nc.sync.dma_start(planes[32 * d : 32 * d + 4, :, 0 : PLANE_BYTES // 4], staged[32 + 16 * d : 48 + 16 * d, :])
 
         load_c(0)
         load_words(last)

@@ -117,13 +117,13 @@ def tile_list_tabhs_d_none_kernel(tc, tab, w4_words, w4_scales, c, u, wgo, offs,
         halves = ((GROUP // 2, GROUP), (0, GROUP // 2))
         last = PASSES - 1
 
-        nc.sync.dma_start(u_raw[:], u.rearrange("(p i) n -> p i n", i=4))
         nc.sync.dma_start(pick[:], offs)
         nc.scalar.dma_start(
             scale_rows[32:96, :], tab[:, 512 * T : 528 * T].bitcast(I32).rearrange("a (q t) -> q a t", q=16)
         )
         nc.scalar.dma_start(staged[32:96, S // 4 :], w4_scales.bitcast(I32).rearrange("a q n -> q a n"))
         load_words(0)
+        nc.sync.dma_start(u_raw[:], u.rearrange("(p i) n -> p i n", i=4))
         load_words(1)
         nc.sync.dma_start(w4[:], w4_words.rearrange("a p b -> p a b").bitcast(I32))
         load_words(2)

from contextlib import ExitStack

import concourse.mybir as mybir

K, M, T, S, L = 2048, 128, 1024, 512, 512
FLOPS = 2 * (K + L) * M * S

F32 = mybir.dt.float32
BF16 = mybir.dt.bfloat16
I32 = mybir.dt.int32
U32 = mybir.dt.uint32
U16 = mybir.dt.uint16
U8 = mybir.dt.uint8
FP8X4 = mybir.dt.float8_e4m3fn_x4
FP4X4 = mybir.dt.float4_e2m1fn_x4
MULT = mybir.AluOpType.mult

P = 128
PASSES = K // 512
GROUP = 128
GROUPS = S // GROUP
HEAD = 32
MX_ALIGN = 64
DMA_ALIGN = 256
PLANE_BYTES = S + M
PLANE_PITCH = 3 * DMA_ALIGN


def tile_list_tabhs_d_none_kernel(tc, tab, w4_words, w4_scales, c, u, wgo, offs, offs2, out):
    nc = tc.nc
    with ExitStack() as ctx:
        keep = ctx.enter_context(tc.tile_pool(name="keep", bufs=1))
        psum = ctx.enter_context(tc.psum_pool(name="psum", bufs=1))

        pick = keep.tile([P, S // 16], U16, name="pick", align_bytes=DMA_ALIGN)
        place = keep.tile([P, S // 16], U16, name="place", align_bytes=DMA_ALIGN)
        scale_rows = keep.tile([P, T // 4], I32, name="scale_rows", align_bytes=DMA_ALIGN)
        words = [keep.tile([P, T], I32, name=f"words{a}", align_bytes=DMA_ALIGN) for a in range(PASSES)]
        picked_words = [keep.tile([P, S], U32, name=f"picked_words{a}", align_bytes=MX_ALIGN) for a in range(PASSES)]
        picked_scales = keep.tile([P, S], U8, name="picked_scales", align_bytes=MX_ALIGN)
        staged = keep.tile([P, PLANE_BYTES // 4], I32, name="staged", align_bytes=DMA_ALIGN)
        planes = keep.tile([P, PASSES, PLANE_PITCH // 4], I32, name="planes", align_bytes=DMA_ALIGN)
        w4 = keep.tile([P, PASSES, M // 2], I32, name="w4", align_bytes=DMA_ALIGN)
        u_raw = keep.tile([P, 4, M], F32, name="u_raw", align_bytes=DMA_ALIGN)
        u_bf = keep.tile([P, M, 4], BF16, name="u_bf", align_bytes=MX_ALIGN)
        u_codes = keep.tile([P, M], U32, name="u_codes", align_bytes=MX_ALIGN)
        u_plane = keep.tile([P, M], U8, name="u_plane", align_bytes=MX_ALIGN)
        c_held = [keep.tile([P, 5 * GROUP], F32, name=f"c_held{g}", align_bytes=DMA_ALIGN) for g in range(GROUPS)]
        c_raw = [t[:, GROUP:].rearrange("p (i w) -> p i w", i=4) for t in c_held]
        c_bf = [keep.tile([P, GROUP, 4], BF16, name=f"c_bf{g}", align_bytes=MX_ALIGN) for g in range(GROUPS)]
        c_codes = [keep.tile([P, GROUP], U32, name=f"c_codes{g}", align_bytes=MX_ALIGN) for g in range(GROUPS)]
        c_plane = [keep.tile([P, GROUP], U8, name=f"c_plane{g}", align_bytes=MX_ALIGN) for g in range(GROUPS)]
        last_sums = keep.tile([P, 2 * GROUP], F32, name="last_sums")
        weights = keep.tile([P, S], F32, name="weights", align_bytes=DMA_ALIGN)
        placed = keep.tile([P, T], F32, name="placed", align_bytes=DMA_ALIGN)
        acc = [psum.tile([M, GROUP], F32, name=f"acc{g}", tag=f"bank{g}") for g in range(GROUPS - 1)]
        c_rows = c.rearrange("(p i) w -> p i w", i=4)

        def load_words(a):
            nc.sync.dma_start(words[a][:], tab[a, 0 : 512 * T].rearrange("(p w) -> p w", p=P).bitcast(I32))

        def load_c(g, lo=0, hi=GROUP):
            nc.sync.dma_start(c_raw[g][:, :, lo:hi], c_rows[:, :, g * GROUP + lo : g * GROUP + hi])

        def load_weights(lo, hi):
            nc.sync.dma_start(weights[:, lo:hi], wgo[:, lo:hi])

        def interleave(dst, src):
            nc.scalar.copy(dst.rearrange("p (w e) i -> p w i e", e=4), src.rearrange("p i (w e) -> p w i e", e=4))

        def quantize(codes, plane, src):
            nc.vector.quantize_mx(out=codes[:].bitcast(FP8X4), scales=plane[:], in_=src[:].rearrange("p w i -> p (w i)"))

        def prepare_c(g, pieces):
            for lo, hi in pieces:
                interleave(c_bf[g][:, lo:hi, :], c_raw[g][:, :, lo:hi])
            quantize(c_codes[g], c_plane[g], c_bf[g])

        def sums_over_head(g):
            return c_held[g][:, HEAD : HEAD + GROUP]

        def gather_words(a, lo, hi):
            nc.vector.tensor_copy(picked_words[a][:, lo:hi], words[a][:].bitcast(U32).indirect(pick[:, lo // 16 : hi // 16]))

        def table_pass(a, g, start, stop):
            cols = slice(g * GROUP, (g + 1) * GROUP)
            plane = planes[:, a, :].bitcast(U8)
            nc.tensor.matmul_mx(
                out=acc[g][:],
                lhsT=w4[:, a, :].bitcast(U8).bitcast(FP4X4),
                lhsT_scale=plane[:, S:PLANE_BYTES],
                rhs=picked_words[a][:, cols].bitcast(FP8X4),
                rhs_scale=plane[:, cols],
                start=start,
                stop=stop,
            )

        def feature_pass(g, stop):
            nc.tensor.matmul_mx(
                out=acc[g][:],
                lhsT=u_codes[:].bitcast(FP8X4),
                lhsT_scale=u_plane[:],
                rhs=c_codes[g][:].bitcast(FP8X4),
                rhs_scale=c_plane[g][:],
                start=False,
                stop=stop,
            )

        def place_sums(held, groups):
            for n, g in enumerate(groups):
                nc.scalar.copy(held[:, n * GROUP : (n + 1) * GROUP], acc[g][:])
            lo, hi = groups[0] * GROUP, (groups[-1] + 1) * GROUP
            nc.vector.tensor_tensor(placed[:].indirect(place[:, lo // 16 : hi // 16]), held, weights[:, lo:hi], MULT)

        whole = ((0, GROUP),)
        head_first = ((0, HEAD), (HEAD, GROUP))
        halves = ((GROUP // 2, GROUP), (0, GROUP // 2))
        last = PASSES - 1

        nc.sync.dma_start(pick[:], offs)
        nc.scalar.dma_start(
            scale_rows[32:96, :], tab[:, 512 * T : 528 * T].bitcast(I32).rearrange("a (q t) -> q a t", q=16)
        )
        nc.scalar.dma_start(staged[32:96, S // 4 :], w4_scales.bitcast(I32).rearrange("a q n -> q a n"))
        load_words(0)
        nc.sync.dma_start(u_raw[:], u.rearrange("(p i) n -> p i n", i=4))
        load_words(1)
        nc.sync.dma_start(w4[:], w4_words.rearrange("a p b -> p a b").bitcast(I32))
        load_words(2)

        nc.vector.memset(scale_rows[0:32, :], 0)
        nc.vector.memset(scale_rows[96:128, :], 0)
        nc.vector.memset(planes[:, :, 0 : PLANE_BYTES // 4], 0)
        nc.vector.memset(placed[:], 0.0)

        nc.vector.tensor_copy(picked_scales[:], scale_rows[:].bitcast(U8).indirect(pick[:]))
        nc.vector.tensor_copy(staged[:, 0 : S // 4], picked_scales[:].bitcast(I32))
        for d in (0, 2, 1, 3):
            nc.sync.dma_start(planes[32 * d : 32 * d + 4, :, 0 : PLANE_BYTES // 4], staged[32 + 16 * d : 48 + 16 * d, :])

        load_c(0)
        load_words(last)
        for lo, hi in halves:
            load_c(1, lo, hi)
        nc.sync.dma_start(place[:], offs2)
        load_weights(0, GROUP)
        load_c(2)
        load_c(3)
        load_weights(GROUP, S)

        for a in range(last):
            gather_words(a, 0, S)
        interleave(u_bf[:], u_raw[:])
        quantize(u_codes, u_plane, u_bf)
        prepare_c(0, whole)
        for g in range(GROUPS - 1):
            for a in range(last):
                table_pass(a, g, a == 0, False)
        feature_pass(0, False)

        gather_words(last, 0, GROUP)
        gather_words(last, GROUP, S)
        table_pass(last, 0, False, True)
        prepare_c(1, halves)
        table_pass(last, 1, False, False)
        feature_pass(1, True)
        table_pass(last, 2, False, False)
        place_sums(sums_over_head(1), (0,))

        acc.append(psum.tile([M, GROUP], F32, name="acc_last", tag="bank0"))
        for a in range(PASSES):
            table_pass(a, 3, a == 0, False)

        for g, pieces in ((2, whole), (3, head_first)):
            prepare_c(g, pieces)
            feature_pass(g, True)
        place_sums(sums_over_head(3), (1,))
        place_sums(last_sums[:], (2, 3))
        nc.sync.dma_start(out, placed[:])
